import numpy as np
CORES = [21,29,37,45,53,61,69,77,85]
N = 9
R, TK = 8, 512
def setup_inputs(rng):
    v = (rng.standard_normal((N, 128, R), dtype=np.float32) / np.float32(np.sqrt(128 * N)))
    return {"x": rng.standard_normal((N, 128, TK), dtype=np.float32), "v": v, "vt": v.transpose(0, 2, 1).copy()}
def setup_inputs_big(rng):
    d = setup_inputs(rng)
    for k in ("x",): d[k] = (d[k].astype(np.float32) * 1048576.0).astype(d[k].dtype)
    return d
def setup_inputs_small(rng):
    d = setup_inputs(rng)
    for k in ("x",): d[k] = (d[k].astype(np.float32) * (1 / 1048576.0)).astype(d[k].dtype)
    return d
def setup_inputs_apart(rng):
    d = setup_inputs(rng)
    f = (10.0 ** rng.permutation(np.linspace(-1.5, 1.5, N))).astype(np.float32).reshape(N, 1, 1)
    for k in ("x",): d[k] = (d[k].astype(np.float32) * f).astype(d[k].dtype)
    return d
def reference(x, v, vt):
    X, V, VT = x.astype(np.float64), v.astype(np.float64), vt.astype(np.float64)
    t = sum(V[j].T @ X[j] for j in range(N))
    return {"y": np.stack([X[r] - 2.0 * (VT[r].T @ t) for r in range(N)]).astype(np.float32)}

@@ -1,0 +1,181 @@
+from concourse.bass import DstId, RemoteDMATransfer
+from concourse.mybir import AluOpType
+
+H = 3
+NE_RANK = 8
+NE_HUB = 8
+R = 8
+C = 512
+P = 128
+NB = C // P
+B = NB * R
+HALF = C // 2
+
+SCRATCH = {
+    "xs": ("sbuf", [P, C], "float32"),
+    "vs": ("sbuf", [P, R], "float32"),
+    "mine": ("sbuf", [P, B], "float32"),
+    "land": ("sbuf", [P, 8 * B], "float32"),
+    "recv": ("sbuf", [P, 2 * B], "float32"),
+    "ts": ("sbuf", [P, B], "float32"),
+    "seed": ("sbuf", [P, P + 1], "float32"),
+    "idd": ("dram", [P + 1, P], "float32"),
+    "eye": ("sbuf", [P, P], "float32"),
+    "w0": ("sbuf", [P, C], "float32"),
+    "tb": ("sbuf", [P, P], "float32"),
+    "ys": ("sbuf", [P, C], "float32"),
+    "ps_t": ("psum", [P, 512], "float32"),
+    "ps_tr": ("psum", [P, 512], "float32"),
+    "ps_y0": ("psum", [P, 512], "float32"),
+    "ps_y1": ("psum", [P, 512], "float32"),
+}
+SEMAPHORES = ["s_v", "s_x0", "s_x1", "s_msa", "s_msw", "s_id1", "s_id2", "s_w", "s_pt", "s_mine", "s_sent", "s_arr",
+              "s_got", "s_ts", "s_ptr", "s_tb", "s_py0", "s_py1", "s_y0", "s_y1", "s_st0", "s_st1"]
+
+
+def _engines(mask, n):
+    bits = [b for b in range(mask.bit_length()) if (mask >> b) & 1]
+    step = len(bits) // n
+    out = 0
+    for b in bits[::step][:n]:
+        out |= 1 << b
+    return out
+
+
+def _common_mask(topo, src, dsts, n):
+    m = topo.mask(src, dsts[0])
+    for d in dsts[1:]:
+        m &= topo.mask(src, d)
+    return _engines(m, n)
+
+
+def _ids(topo, cores):
+    out = []
+    for c in cores:
+        rid, pid, _se = topo.addr(c)
+        out.append(DstId(rid=rid, pnc=pid))
+    return out
+
+
+def _plan(T, topo):
+    ranks = list(T.cores)
+    groups = []
+    for c in ranks:
+        for grp in groups:
+            if topo.may_write(c, grp[0]) and topo.may_write(grp[0], c):
+                grp.append(c)
+                break
+        else:
+            groups.append([c])
+    every = range(topo.CHIPS * topo.CORES_PER_CHIP)
+    plan = []
+    for grp in groups:
+        n = len(grp)
+        homes = [grp[(i * (n - 1)) // (H - 1)] for i in range(H)] if H > 1 else [grp[n // 2]]
+        hubs = []
+        for home in homes:
+            ok = [c for c in every
+                  if topo.chip(c) == topo.chip(home) and topo.die(c) == topo.die(home) and c not in ranks
+                  and all(topo.may_write(c, d) for d in ranks) and all(topo.may_write(s, c) for s in grp)]
+            hubs.append(ok[0])
+        share = {h: [] for h in hubs}
+        rest = []
+        for d in ranks:
+            near = [h for h in hubs
+                    if topo.chip(h) == topo.chip(d) or topo.mates(topo.chip(h), topo.chip(d))]
+            if near:
+                share[near[0]].append(d)
+            else:
+                rest.append(d)
+        for d in rest:
+            share[min(hubs, key=lambda q: len(share[q]))].append(d)
+        plan.append((grp, hubs, share))
+    return plan
+
+
+def _hub_program(g, core, T, topo, gi, grp, dests):
+    S = T.sem
+    g.wait_ge(S.s_arr, NE_RANK * len(grp))
+    g.remote_dma_fused(
+        [RemoteDMATransfer(dst_ids=_ids(topo, dests), dma_engine_mask=_common_mask(topo, core, dests, NE_HUB),
+                           remote_sem=S.s_got, srcs=[T.land[:, B * i:B * (i + 1)] for i in range(len(grp))],
+                           dsts=[T.recv[:, B * gi:B * (gi + 1)] for _d in dests], alu_op=1)],
+        local_sem=S.s_sent)
+    g.wait_ge(S.s_sent, NE_HUB)
+
+
+def rank_program(g, core, T, topo):
+    plan = _plan(T, topo)
+    for gi, (grp, hubs, share) in enumerate(plan):
+        if core in hubs:
+            _hub_program(g, core, T, topo, gi, grp, share[core])
+            return
+    if T.rank_of(core) is None:
+        return
+    S = T.sem
+    grp, hubs = [(a, b) for (a, b, _c) in plan if core in a][0]
+    slot = grp.index(core)
+    sy, sc, ve, pe = g.sync, g.scalar, g.vector, g.tensor
+
+    sc.dma_start(T.xs[:, 0:HALF], T.x[:, 0:HALF]).then_inc(S.s_x0, 16)
+    sy.dma_start(T.vs[:, :], T.v[:, :]).then_inc(S.s_v, 16)
+    sy.dma_start(T.xs[:, HALF:C], T.x[:, HALF:C]).then_inc(S.s_x1, 16)
+
+    ve.memset(T.seed[:, 0:1], -2.0).then_inc(S.s_msa, 1)
+    ve.memset(T.seed[:, 1:P + 1], 0.0).then_inc(S.s_msa, 1)
+    ve.memset(T.w0[0:B, :], 0.0).then_inc(S.s_msw, 1)
+    sy.wait_ge(S.s_msw, 1)
+    sc.wait_ge(S.s_msw, 1)
+    for k in range(NB):
+        q = sc if k % 2 == 0 else sy
+        q.dma_start(T.w0[R * k:R * (k + 1), P * k:P * (k + 1)], T.vt[:, :]).then_inc(S.s_w, 16)
+    sy.wait_ge(S.s_msa, 2)
+    sy.dma_start(T.idd[:, :], T.seed[:, :]).then_inc(S.s_id1, 16)
+    sy.wait_ge(S.s_id1, 16)
+    sy.dma_start(T.eye[:, :], T.idd[0:P, :]).then_inc(S.s_id2, 16)
+
+    pe.wait_ge(S.s_v, 16)
+    pe.wait_ge(S.s_x0, 16)
+    for k in range(NB):
+        if k == NB // 2:
+            pe.wait_ge(S.s_x1, 16)
+        pe.matmul(out=T.ps_t[:, R * k:R * (k + 1)], lhsT=T.xs[:, P * k:P * (k + 1)], rhs=T.vs[:, :],
+                  start=True, stop=True).then_inc(S.s_pt, 1)
+    ve.wait_ge(S.s_pt, NB)
+    ve.tensor_copy(out=T.mine[:, :], in_=T.ps_t[:, 0:B]).then_inc(S.s_mine, 1)
+
+    g.wait_ge(S.s_mine, 1)
+    g.remote_dma_fused(
+        [RemoteDMATransfer(dst_ids=_ids(topo, hubs), dma_engine_mask=_common_mask(topo, core, hubs, NE_RANK),
+                           remote_sem=S.s_arr, srcs=[T.mine[:, :]],
+                           dsts=[T.land[:, B * slot:B * (slot + 1)] for _h in hubs], alu_op=0)],
+        local_sem=S.s_sent)
+    g.wait_ge(S.s_sent, NE_RANK)
+
+    ve.wait_ge(S.s_got, NE_HUB * len(plan))
+    ve.tensor_tensor(out=T.ts[:, :], in0=T.recv[:, 0:B], in1=T.recv[:, B:2 * B], op=AluOpType.add).then_inc(S.s_ts, 1)
+    pe.wait_ge(S.s_id2, 16)
+    pe.wait_ge(S.s_ts, 1)
+    pe.matmul(out=T.ps_tr[0:B, 0:P], lhsT=T.ts[:, :], rhs=T.eye[:, :], start=True, stop=True).then_inc(S.s_ptr, 1)
+    ve.wait_ge(S.s_ptr, 1)
+    ve.tensor_copy(out=T.tb[0:B, :], in_=T.ps_tr[0:B, 0:P]).then_inc(S.s_tb, 1)
+
+    pe.wait_ge(S.s_w, 16 * NB)
+    pe.wait_ge(S.s_tb, 1)
+    ps_y = [T.ps_y0, T.ps_y1]
+    s_py = [S.s_py0, S.s_py1]
+    s_y = [S.s_y0, S.s_y1]
+    s_st = [S.s_st0, S.s_st1]
+    for k in range(NB):
+        hf, o = divmod(k, NB // 2)
+        pe.matmul(out=ps_y[hf][:, P * o:P * (o + 1)], lhsT=T.w0[0:B, P * k:P * (k + 1)], rhs=T.tb[0:B, :],
+                  start=True, stop=True).then_inc(s_py[hf], 1)
+    ve.wait_ge(S.s_x0, 16)
+    ve.wait_ge(S.s_x1, 16)
+    for hf, q in enumerate((sy, sc)):
+        ve.wait_ge(s_py[hf], NB // 2)
+        ve.tensor_tensor(out=T.ys[:, HALF * hf:HALF * (hf + 1)], in0=T.xs[:, HALF * hf:HALF * (hf + 1)],
+                         in1=ps_y[hf][:, 0:HALF], op=AluOpType.add).then_inc(s_y[hf], 1)
+        q.wait_ge(s_y[hf], 1)
+        q.dma_start(T.y[:, HALF * hf:HALF * (hf + 1)], T.ys[:, HALF * hf:HALF * (hf + 1)]).then_inc(s_st[hf], 16)
+        q.wait_ge(s_st[hf], 16)

@@ -10,6 +10,7 @@ P = 128
 NB = C // P
 B = NB * R
 HALF = C // 2
+E = P // 2
 
 SCRATCH = {
     "xs": ("sbuf", [P, C], "float32"),
@@ -18,8 +19,8 @@ SCRATCH = {
     "land": ("sbuf", [P, 8 * B], "float32"),
     "recv": ("sbuf", [P, 2 * B], "float32"),
     "ts": ("sbuf", [P, B], "float32"),
-    "seed": ("sbuf", [P, P + 1], "float32"),
-    "idd": ("dram", [P + 1, P], "float32"),
+    "seed": ("sbuf", [P, E + 1], "float32"),
+    "idd": ("dram", [P + 2, E], "float32"),
     "eye": ("sbuf", [P, P], "float32"),
     "w0": ("sbuf", [P, C], "float32"),
     "tb": ("sbuf", [P, P], "float32"),
@@ -95,13 +96,25 @@ def _plan(T, topo):
 
 def _hub_program(g, core, T, topo, gi, grp, dests):
     S = T.sem
+    ids = _ids(topo, dests)
+    mask = _common_mask(topo, core, dests, NE_HUB)
+    g.vector.memset(T.seed[:, 1:E + 1], 0.0).then_inc(S.s_msa, 1)
+    for i in range(P // E):
+        g.vector.memset(T.seed[E * i:E * (i + 1), 0:1], -2.0 if i == gi else 0.0).then_inc(S.s_msa, 1)
+    g.sync.wait_ge(S.s_msa, 1 + P // E)
+    g.sync.dma_start(T.idd[:, :], T.seed[:, :]).then_inc(S.s_id1, 16)
+    g.wait_ge(S.s_id1, 16)
+    g.remote_dma_fused(
+        [RemoteDMATransfer(dst_ids=ids, dma_engine_mask=mask, remote_sem=S.s_id2, srcs=[T.idd[gi:gi + P, :]],
+                           dsts=[T.eye[:, E * gi:E * (gi + 1)] for _d in dests], alu_op=0)],
+        local_sem=S.s_sent)
     g.wait_ge(S.s_arr, NE_RANK * len(grp))
     g.remote_dma_fused(
-        [RemoteDMATransfer(dst_ids=_ids(topo, dests), dma_engine_mask=_common_mask(topo, core, dests, NE_HUB),
-                           remote_sem=S.s_got, srcs=[T.land[:, B * i:B * (i + 1)] for i in range(len(grp))],
+        [RemoteDMATransfer(dst_ids=ids, dma_engine_mask=mask, remote_sem=S.s_got,
+                           srcs=[T.land[:, B * i:B * (i + 1)] for i in range(len(grp))],
                            dsts=[T.recv[:, B * gi:B * (gi + 1)] for _d in dests], alu_op=1)],
         local_sem=S.s_sent)
-    g.wait_ge(S.s_sent, NE_HUB)
+    g.wait_ge(S.s_sent, 2 * NE_HUB)
 
 
 def rank_program(g, core, T, topo):
@@ -121,18 +134,12 @@ def rank_program(g, core, T, topo):
     sy.dma_start(T.vs[:, :], T.v[:, :]).then_inc(S.s_v, 16)
     sy.dma_start(T.xs[:, HALF:C], T.x[:, HALF:C]).then_inc(S.s_x1, 16)
 
-    ve.memset(T.seed[:, 0:1], -2.0).then_inc(S.s_msa, 1)
-    ve.memset(T.seed[:, 1:P + 1], 0.0).then_inc(S.s_msa, 1)
     ve.memset(T.w0[0:B, :], 0.0).then_inc(S.s_msw, 1)
     sy.wait_ge(S.s_msw, 1)
     sc.wait_ge(S.s_msw, 1)
     for k in range(NB):
         q = sc if k % 2 == 0 else sy
         q.dma_start(T.w0[R * k:R * (k + 1), P * k:P * (k + 1)], T.vt[:, :]).then_inc(S.s_w, 16)
-    sy.wait_ge(S.s_msa, 2)
-    sy.dma_start(T.idd[:, :], T.seed[:, :]).then_inc(S.s_id1, 16)
-    sy.wait_ge(S.s_id1, 16)
-    sy.dma_start(T.eye[:, :], T.idd[0:P, :]).then_inc(S.s_id2, 16)
 
     pe.wait_ge(S.s_v, 16)
     pe.wait_ge(S.s_x0, 16)
@@ -154,7 +161,7 @@ def rank_program(g, core, T, topo):
 
     ve.wait_ge(S.s_got, NE_HUB * len(plan))
     ve.tensor_tensor(out=T.ts[:, :], in0=T.recv[:, 0:B], in1=T.recv[:, B:2 * B], op=AluOpType.add).then_inc(S.s_ts, 1)
-    pe.wait_ge(S.s_id2, 16)
+    pe.wait_ge(S.s_id2, NE_HUB * len(plan))
     pe.wait_ge(S.s_ts, 1)
     pe.matmul(out=T.ps_tr[0:B, 0:P], lhsT=T.ts[:, :], rhs=T.eye[:, :], start=True, stop=True).then_inc(S.s_ptr, 1)
     ve.wait_ge(S.s_ptr, 1)

@@ -7,10 +7,17 @@ NE_HUB = 8
 R = 8
 C = 512
 P = 128
-NB = C // P
-B = NB * R
-HALF = C // 2
-E = P // 2
+Q = 32
+NA = P // Q
+NU = 2
+NBK = 2
+B = NBK * NU * R
+UR = NU * R
+HALF = C // NU
+RUN = NBK * Q
+PAD = RUN // B
+NZ = C // RUN
+PIECES = 4
 
 SCRATCH = {
     "xs": ("sbuf", [P, C], "float32"),
@@ -18,20 +25,17 @@ SCRATCH = {
     "mine": ("sbuf", [P, B], "float32"),
     "land": ("sbuf", [P, 8 * B], "float32"),
     "recv": ("sbuf", [P, 2 * B], "float32"),
-    "ts": ("sbuf", [P, B], "float32"),
-    "seed": ("sbuf", [P, E + 1], "float32"),
-    "idd": ("dram", [P + 2, E], "float32"),
-    "eye": ("sbuf", [P, P], "float32"),
-    "w0": ("sbuf", [P, C], "float32"),
-    "tb": ("sbuf", [P, P], "float32"),
+    "seed": ("sbuf", [P, Q], "float32"),
+    "ts": ("sbuf", [P, RUN], "float32"),
+    "tt": ("sbuf", [P, RUN], "float32"),
+    "wt": ("sbuf", [P, NU * P], "float32"),
     "ys": ("sbuf", [P, C], "float32"),
-    "ps_t": ("psum", [P, 512], "float32"),
-    "ps_tr": ("psum", [P, 512], "float32"),
-    "ps_y0": ("psum", [P, 512], "float32"),
-    "ps_y1": ("psum", [P, 512], "float32"),
 }
-SEMAPHORES = ["s_v", "s_x0", "s_x1", "s_msa", "s_msw", "s_id1", "s_id2", "s_w", "s_pt", "s_mine", "s_sent", "s_arr",
-              "s_got", "s_ts", "s_ptr", "s_tb", "s_py0", "s_py1", "s_y0", "s_y1", "s_st0", "s_st1"]
+for _z in range(NZ):
+    SCRATCH["ps%d" % _z] = ("psum", [P, 512], "float32")
+SEMAPHORES = (["s_v", "s_x0", "s_x1", "s_msa", "s_msw", "s_pad", "s_w", "s_pt", "s_mine", "s_sent", "s_arr",
+               "s_got", "s_ts", "s_tt"] + ["s_p%d" % z for z in range(NZ)]
+              + ["s_y%d" % k for k in range(PIECES)] + ["s_st%d" % k for k in range(PIECES)])
 
 
 def _engines(mask, n):
@@ -98,15 +102,11 @@ def _hub_program(g, core, T, topo, gi, grp, dests):
     S = T.sem
     ids = _ids(topo, dests)
     mask = _common_mask(topo, core, dests, NE_HUB)
-    g.vector.memset(T.seed[:, 1:E + 1], 0.0).then_inc(S.s_msa, 1)
-    for i in range(P // E):
-        g.vector.memset(T.seed[E * i:E * (i + 1), 0:1], -2.0 if i == gi else 0.0).then_inc(S.s_msa, 1)
-    g.sync.wait_ge(S.s_msa, 1 + P // E)
-    g.sync.dma_start(T.idd[:, :], T.seed[:, :]).then_inc(S.s_id1, 16)
-    g.wait_ge(S.s_id1, 16)
+    g.vector.memset(T.seed[:, :], 0.0).then_inc(S.s_msa, 1)
+    g.wait_ge(S.s_msa, 1)
     g.remote_dma_fused(
-        [RemoteDMATransfer(dst_ids=ids, dma_engine_mask=mask, remote_sem=S.s_id2, srcs=[T.idd[gi:gi + P, :]],
-                           dsts=[T.eye[:, E * gi:E * (gi + 1)] for _d in dests], alu_op=0)],
+        [RemoteDMATransfer(dst_ids=ids, dma_engine_mask=mask, remote_sem=S.s_pad, srcs=[T.seed[:, :]],
+                           dsts=[T.ts[:, Q * gi:Q * (gi + 1)] for _d in dests], alu_op=0)],
         local_sem=S.s_sent)
     g.wait_ge(S.s_arr, NE_RANK * len(grp))
     g.remote_dma_fused(
@@ -129,27 +129,31 @@ def rank_program(g, core, T, topo):
     grp, hubs = [(a, b) for (a, b, _c) in plan if core in a][0]
     slot = grp.index(core)
     sy, sc, ve, pe = g.sync, g.scalar, g.vector, g.tensor
+    ps_t = T["ps%d" % (NZ - 1)]
 
     sc.dma_start(T.xs[:, 0:HALF], T.x[:, 0:HALF]).then_inc(S.s_x0, 16)
     sy.dma_start(T.vs[:, :], T.v[:, :]).then_inc(S.s_v, 16)
     sy.dma_start(T.xs[:, HALF:C], T.x[:, HALF:C]).then_inc(S.s_x1, 16)
 
-    ve.memset(T.w0[0:B, :], 0.0).then_inc(S.s_msw, 1)
+    ve.memset(T.wt[:, :], 0.0).then_inc(S.s_msw, 1)
     sy.wait_ge(S.s_msw, 1)
     sc.wait_ge(S.s_msw, 1)
-    for k in range(NB):
-        q = sc if k % 2 == 0 else sy
-        q.dma_start(T.w0[R * k:R * (k + 1), P * k:P * (k + 1)], T.vt[:, :]).then_inc(S.s_w, 16)
+    for a in range(NA):
+        for u in range(NU):
+            q = sc if u == 0 else sy
+            q.dma_start(T.wt[Q * a + PAD * R * u:Q * a + PAD * R * (u + 1):PAD, P * u:P * (u + 1)],
+                        T.vt[:, :]).then_inc(S.s_w, 16)
 
     pe.wait_ge(S.s_v, 16)
-    pe.wait_ge(S.s_x0, 16)
-    for k in range(NB):
-        if k == NB // 2:
-            pe.wait_ge(S.s_x1, 16)
-        pe.matmul(out=T.ps_t[:, R * k:R * (k + 1)], lhsT=T.xs[:, P * k:P * (k + 1)], rhs=T.vs[:, :],
-                  start=True, stop=True).then_inc(S.s_pt, 1)
-    ve.wait_ge(S.s_pt, NB)
-    ve.tensor_copy(out=T.mine[:, :], in_=T.ps_t[:, 0:B]).then_inc(S.s_mine, 1)
+    for u in range(NU):
+        pe.wait_ge(S.s_x0 if u == 0 else S.s_x1, 16)
+        for b in range(NBK):
+            o = UR * b + R * u
+            pe.matmul(out=ps_t[:, o:o + R], lhsT=T.xs[:, HALF * u + b:HALF * (u + 1):NBK], rhs=T.vs[:, :],
+                      start=True, stop=True).then_inc(S.s_pt, 1)
+    ve.wait_ge(S.s_pt, NU * NBK)
+    ve.tensor_scalar(out=T.mine[:, :], in0=ps_t[:, 0:B], scalar1=-2.0, scalar2=None,
+                     op0=AluOpType.mult).then_inc(S.s_mine, 1)
 
     g.wait_ge(S.s_mine, 1)
     g.remote_dma_fused(
@@ -159,30 +163,34 @@ def rank_program(g, core, T, topo):
         local_sem=S.s_sent)
     g.wait_ge(S.s_sent, NE_RANK)
 
+    ve.wait_ge(S.s_pad, NE_HUB * len(plan))
     ve.wait_ge(S.s_got, NE_HUB * len(plan))
-    ve.tensor_tensor(out=T.ts[:, :], in0=T.recv[:, 0:B], in1=T.recv[:, B:2 * B], op=AluOpType.add).then_inc(S.s_ts, 1)
-    pe.wait_ge(S.s_id2, NE_HUB * len(plan))
-    pe.wait_ge(S.s_ts, 1)
-    pe.matmul(out=T.ps_tr[0:B, 0:P], lhsT=T.ts[:, :], rhs=T.eye[:, :], start=True, stop=True).then_inc(S.s_ptr, 1)
-    ve.wait_ge(S.s_ptr, 1)
-    ve.tensor_copy(out=T.tb[0:B, :], in_=T.ps_tr[0:B, 0:P]).then_inc(S.s_tb, 1)
+    ve.tensor_tensor(out=T.ts[:, 0:RUN:PAD], in0=T.recv[:, 0:B], in1=T.recv[:, B:2 * B],
+                     op=AluOpType.add).then_inc(S.s_ts, 1)
+    ve.wait_ge(S.s_ts, 1)
+    ve.transpose(out=T.tt[:, :], in_=T.ts[:, :]).then_inc(S.s_tt, 1)
 
-    pe.wait_ge(S.s_w, 16 * NB)
-    pe.wait_ge(S.s_tb, 1)
-    ps_y = [T.ps_y0, T.ps_y1]
-    s_py = [S.s_py0, S.s_py1]
-    s_y = [S.s_y0, S.s_y1]
-    s_st = [S.s_st0, S.s_st1]
-    for k in range(NB):
-        hf, o = divmod(k, NB // 2)
-        pe.matmul(out=ps_y[hf][:, P * o:P * (o + 1)], lhsT=T.w0[0:B, P * k:P * (k + 1)], rhs=T.tb[0:B, :],
-                  start=True, stop=True).then_inc(s_py[hf], 1)
+    pe.wait_ge(S.s_w, 16 * NA * NU)
+    pe.wait_ge(S.s_mine, 1)
+    pe.wait_ge(S.s_tt, 1)
+    for z in range(NZ):
+        u, a = divmod(z, NA)
+        pe.matmul(out=T["ps%d" % z][:, 0:RUN], lhsT=T.wt[Q * a:Q * (a + 1), P * u:P * (u + 1)],
+                  rhs=T.tt[Q * a:Q * (a + 1), :], start=True, stop=True).then_inc(S["s_p%d" % z], 1)
     ve.wait_ge(S.s_x0, 16)
     ve.wait_ge(S.s_x1, 16)
-    for hf, q in enumerate((sy, sc)):
-        ve.wait_ge(s_py[hf], NB // 2)
-        ve.tensor_tensor(out=T.ys[:, HALF * hf:HALF * (hf + 1)], in0=T.xs[:, HALF * hf:HALF * (hf + 1)],
-                         in1=ps_y[hf][:, 0:HALF], op=AluOpType.add).then_inc(s_y[hf], 1)
-        q.wait_ge(s_y[hf], 1)
-        q.dma_start(T.y[:, HALF * hf:HALF * (hf + 1)], T.ys[:, HALF * hf:HALF * (hf + 1)]).then_inc(s_st[hf], 16)
-        q.wait_ge(s_st[hf], 16)
+    per = NZ // PIECES
+    w = C // PIECES
+    for z in range(NZ):
+        k = z // per
+        ve.wait_ge(S["s_p%d" % z], 1)
+        for b in range(NBK):
+            ve.tensor_tensor(out=T.ys[:, RUN * z + b:RUN * (z + 1):NBK], in0=T.xs[:, RUN * z + b:RUN * (z + 1):NBK],
+                             in1=T["ps%d" % z][:, Q * b:Q * (b + 1)], op=AluOpType.add).then_inc(S["s_y%d" % k], 1)
+    for k in range(PIECES):
+        q = sy if k % 2 == 0 else sc
+        q.wait_ge(S["s_y%d" % k], per * NBK)
+        q.dma_start(T.y[:, w * k:w * (k + 1)], T.ys[:, w * k:w * (k + 1)]).then_inc(S["s_st%d" % k], 16)
+    for k in range(PIECES):
+        q = sy if k % 2 == 0 else sc
+        q.wait_ge(S["s_st%d" % k], 16)

@@ -98,15 +98,16 @@ def _plan(T, topo):
     return plan
 
 
-def _hub_program(g, core, T, topo, gi, grp, dests):
+def _hub_program(g, core, T, topo, gi, ng, grp, dests):
     S = T.sem
     ids = _ids(topo, dests)
     mask = _common_mask(topo, core, dests, NE_HUB)
-    g.vector.memset(T.seed[:, :], 0.0).then_inc(S.s_msa, 1)
+    hp = Q // ng
+    g.vector.memset(T.seed[:, 0:hp], 0.0).then_inc(S.s_msa, 1)
     g.wait_ge(S.s_msa, 1)
     g.remote_dma_fused(
-        [RemoteDMATransfer(dst_ids=ids, dma_engine_mask=mask, remote_sem=S.s_pad, srcs=[T.seed[:, :]],
-                           dsts=[T.ts[:, Q * gi:Q * (gi + 1)] for _d in dests], alu_op=0)],
+        [RemoteDMATransfer(dst_ids=ids, dma_engine_mask=mask, remote_sem=S.s_pad, srcs=[T.seed[:, 0:hp]],
+                           dsts=[T.ts[:, hp * gi:hp * (gi + 1)] for _d in dests], alu_op=0)],
         local_sem=S.s_sent)
     g.wait_ge(S.s_arr, NE_RANK * len(grp))
     g.remote_dma_fused(
@@ -121,19 +122,28 @@ def rank_program(g, core, T, topo):
     plan = _plan(T, topo)
     for gi, (grp, hubs, share) in enumerate(plan):
         if core in hubs:
-            _hub_program(g, core, T, topo, gi, grp, share[core])
+            _hub_program(g, core, T, topo, gi, len(plan), grp, share[core])
             return
     if T.rank_of(core) is None:
         return
     S = T.sem
     grp, hubs = [(a, b) for (a, b, _c) in plan if core in a][0]
     slot = grp.index(core)
+    nxt = grp[(slot + 1) % len(grp)]
+    mask = _common_mask(topo, core, hubs + [nxt], NE_RANK)
     sy, sc, ve, pe = g.sync, g.scalar, g.vector, g.tensor
     ps_t = T["ps%d" % (NZ - 1)]
 
     sc.dma_start(T.xs[:, 0:HALF], T.x[:, 0:HALF]).then_inc(S.s_x0, 16)
     sy.dma_start(T.vs[:, :], T.v[:, :]).then_inc(S.s_v, 16)
     sy.dma_start(T.xs[:, HALF:C], T.x[:, HALF:C]).then_inc(S.s_x1, 16)
+
+    ve.memset(T.seed[:, 0:RUN - Q], 0.0).then_inc(S.s_msa, 1)
+    g.wait_ge(S.s_msa, 1)
+    g.remote_dma_fused(
+        [RemoteDMATransfer(dst_ids=_ids(topo, [nxt]), dma_engine_mask=mask, remote_sem=S.s_pad,
+                           srcs=[T.seed[:, 0:RUN - Q]], dsts=[T.ts[:, Q:RUN]], alu_op=0)],
+        local_sem=S.s_sent)
 
     ve.memset(T.wt[:, :], 0.0).then_inc(S.s_msw, 1)
     sy.wait_ge(S.s_msw, 1)
@@ -157,13 +167,13 @@ def rank_program(g, core, T, topo):
 
     g.wait_ge(S.s_mine, 1)
     g.remote_dma_fused(
-        [RemoteDMATransfer(dst_ids=_ids(topo, hubs), dma_engine_mask=_common_mask(topo, core, hubs, NE_RANK),
+        [RemoteDMATransfer(dst_ids=_ids(topo, hubs), dma_engine_mask=mask,
                            remote_sem=S.s_arr, srcs=[T.mine[:, :]],
                            dsts=[T.land[:, B * slot:B * (slot + 1)] for _h in hubs], alu_op=0)],
         local_sem=S.s_sent)
-    g.wait_ge(S.s_sent, NE_RANK)
+    g.wait_ge(S.s_sent, 2 * NE_RANK)
 
-    ve.wait_ge(S.s_pad, NE_HUB * len(plan))
+    ve.wait_ge(S.s_pad, NE_HUB * len(plan) + NE_RANK)
     ve.wait_ge(S.s_got, NE_HUB * len(plan))
     ve.tensor_tensor(out=T.ts[:, 0:RUN:PAD], in0=T.recv[:, 0:B], in1=T.recv[:, B:2 * B],
                      op=AluOpType.add).then_inc(S.s_ts, 1)

@@ -1,9 +1,9 @@
 from concourse.bass import DstId, RemoteDMATransfer
 from concourse.mybir import AluOpType
 
-H = 3
-NE_RANK = 8
-NE_HUB = 8
+NS = 4
+NE_ON = 16
+NE_OFF = 8
 R = 8
 C = 512
 P = 128
@@ -11,30 +11,33 @@ Q = 32
 NA = P // Q
 NU = 2
 NBK = 2
-B = NBK * NU * R
-UR = NU * R
+B = NU * NBK * R
 HALF = C // NU
+W = NS * B
 RUN = NBK * Q
-PAD = RUN // B
 NZ = C // RUN
 PIECES = 4
+ZN = Q
+ZH = (W - ZN) // NS
 
 SCRATCH = {
     "xs": ("sbuf", [P, C], "float32"),
     "vs": ("sbuf", [P, R], "float32"),
     "mine": ("sbuf", [P, B], "float32"),
-    "land": ("sbuf", [P, 8 * B], "float32"),
-    "recv": ("sbuf", [P, 2 * B], "float32"),
+    "land": ("sbuf", [P, 2 * NS * B], "float32"),
     "seed": ("sbuf", [P, Q], "float32"),
-    "ts": ("sbuf", [P, RUN], "float32"),
-    "tt": ("sbuf", [P, RUN], "float32"),
-    "wt": ("sbuf", [P, NU * P], "float32"),
+    "to": ("sbuf", [P, W], "float32"),
+    "tto": ("sbuf", [P, W], "float32"),
+    "ts": ("sbuf", [P, W], "float32"),
+    "tt": ("sbuf", [P, W], "float32"),
+    "wt": ("sbuf", [P, P], "float32"),
     "ys": ("sbuf", [P, C], "float32"),
 }
 for _z in range(NZ):
     SCRATCH["ps%d" % _z] = ("psum", [P, 512], "float32")
-SEMAPHORES = (["s_v", "s_x0", "s_x1", "s_msa", "s_msw", "s_pad", "s_w", "s_pt", "s_mine", "s_sent", "s_arr",
-               "s_got", "s_ts", "s_tt"] + ["s_p%d" % z for z in range(NZ)]
+SEMAPHORES = (["s_v", "s_x0", "s_x1", "s_msa", "s_pad", "s_w", "s_pt", "s_mine", "s_sent", "s_arr", "s_to", "s_ts"]
+              + ["s_tto%d" % u for u in range(NU)] + ["s_tt%d" % u for u in range(NU)]
+              + ["s_g%d" % q for q in range(NS)] + ["s_p%d" % z for z in range(NZ)]
               + ["s_y%d" % k for k in range(PIECES)] + ["s_st%d" % k for k in range(PIECES)])
 
 
@@ -62,75 +65,57 @@ def _ids(topo, cores):
     return out
 
 
-def _plan(T, topo):
+def _forwarders(T, topo, c):
     ranks = list(T.cores)
-    groups = []
-    for c in ranks:
-        for grp in groups:
-            if topo.may_write(c, grp[0]) and topo.may_write(grp[0], c):
-                grp.append(c)
-                break
-        else:
-            groups.append([c])
-    every = range(topo.CHIPS * topo.CORES_PER_CHIP)
-    plan = []
-    for grp in groups:
-        n = len(grp)
-        homes = [grp[(i * (n - 1)) // (H - 1)] for i in range(H)] if H > 1 else [grp[n // 2]]
-        hubs = []
-        for home in homes:
-            ok = [c for c in every
-                  if topo.chip(c) == topo.chip(home) and topo.die(c) == topo.die(home) and c not in ranks
-                  and all(topo.may_write(c, d) for d in ranks) and all(topo.may_write(s, c) for s in grp)]
-            hubs.append(ok[0])
-        share = {h: [] for h in hubs}
-        rest = []
-        for d in ranks:
-            near = [h for h in hubs
-                    if topo.chip(h) == topo.chip(d) or topo.mates(topo.chip(h), topo.chip(d))]
-            if near:
-                share[near[0]].append(d)
-            else:
-                rest.append(d)
-        for d in rest:
-            share[min(hubs, key=lambda q: len(share[q]))].append(d)
-        plan.append((grp, hubs, share))
-    return plan
+    ok = [h for h in range(topo.CHIPS * topo.CORES_PER_CHIP)
+          if topo.chip(h) == topo.chip(c) and h not in ranks and topo.may_write(c, h)
+          and all(topo.may_write(h, d) for d in ranks)]
+    near = [h for h in ok if topo.die(h) == topo.die(c)]
+    far = [h for h in ok if topo.die(h) != topo.die(c)]
+    half = NS // 2
+    return near[:half] + far[:NS - half]
 
 
-def _hub_program(g, core, T, topo, gi, ng, grp, dests):
+def _neighbour(T, topo, c):
+    grp = [d for d in T.cores if d == c or (topo.may_write(c, d) and topo.may_write(d, c))]
+    return grp[(grp.index(c) + 1) % len(grp)]
+
+
+def _forwarder_program(g, core, T, topo, home, q):
     S = T.sem
-    ids = _ids(topo, dests)
-    mask = _common_mask(topo, core, dests, NE_HUB)
-    hp = Q // ng
-    g.vector.memset(T.seed[:, 0:hp], 0.0).then_inc(S.s_msa, 1)
+    ranks = list(T.cores)
+    n = len(ranks)
+    i = ranks.index(home)
+    offs = [o for o in range(1, n) if (o - 1) % NS == q]
+    dests = [ranks[(i + o) % n] for o in offs]
+    mask = _common_mask(topo, core, dests + [home], NE_OFF)
+    lo = ZN + ZH * q
+    g.vector.memset(T.seed[:, 0:ZH], 0.0).then_inc(S.s_msa, 1)
     g.wait_ge(S.s_msa, 1)
     g.remote_dma_fused(
-        [RemoteDMATransfer(dst_ids=ids, dma_engine_mask=mask, remote_sem=S.s_pad, srcs=[T.seed[:, 0:hp]],
-                           dsts=[T.ts[:, hp * gi:hp * (gi + 1)] for _d in dests], alu_op=0)],
+        [RemoteDMATransfer(dst_ids=_ids(topo, [home]), dma_engine_mask=mask, remote_sem=S.s_pad,
+                           srcs=[T.seed[:, 0:ZH]], dsts=[T.to[:, lo:lo + ZH]], alu_op=0)],
         local_sem=S.s_sent)
-    g.wait_ge(S.s_arr, NE_RANK * len(grp))
+    g.wait_ge(S.s_arr, NE_ON)
     g.remote_dma_fused(
-        [RemoteDMATransfer(dst_ids=ids, dma_engine_mask=mask, remote_sem=S.s_got,
-                           srcs=[T.land[:, B * i:B * (i + 1)] for i in range(len(grp))],
-                           dsts=[T.recv[:, B * gi:B * (gi + 1)] for _d in dests], alu_op=1)],
+        [RemoteDMATransfer(dst_ids=_ids(topo, dests), dma_engine_mask=mask, remote_sem=S["s_g%d" % q],
+                           srcs=[T.mine[:, :]], dsts=[T.land[:, B * (o - 1):B * o] for o in offs], alu_op=0)],
         local_sem=S.s_sent)
-    g.wait_ge(S.s_sent, 2 * NE_HUB)
+    g.wait_ge(S.s_sent, 2 * NE_OFF)
 
 
 def rank_program(g, core, T, topo):
-    plan = _plan(T, topo)
-    for gi, (grp, hubs, share) in enumerate(plan):
-        if core in hubs:
-            _hub_program(g, core, T, topo, gi, len(plan), grp, share[core])
+    for c in T.cores:
+        if topo.chip(c) == topo.chip(core) and c != core:
+            fw = _forwarders(T, topo, c)
+            if core in fw:
+                _forwarder_program(g, core, T, topo, c, fw.index(core))
             return
     if T.rank_of(core) is None:
         return
     S = T.sem
-    grp, hubs = [(a, b) for (a, b, _c) in plan if core in a][0]
-    slot = grp.index(core)
-    nxt = grp[(slot + 1) % len(grp)]
-    mask = _common_mask(topo, core, hubs + [nxt], NE_RANK)
+    fw = _forwarders(T, topo, core)
+    nxt = _neighbour(T, topo, core)
     sy, sc, ve, pe = g.sync, g.scalar, g.vector, g.tensor
     ps_t = T["ps%d" % (NZ - 1)]
 
@@ -138,27 +123,23 @@ def rank_program(g, core, T, topo):
     sy.dma_start(T.vs[:, :], T.v[:, :]).then_inc(S.s_v, 16)
     sy.dma_start(T.xs[:, HALF:C], T.x[:, HALF:C]).then_inc(S.s_x1, 16)
 
-    ve.memset(T.seed[:, 0:RUN - Q], 0.0).then_inc(S.s_msa, 1)
+    ve.memset(T.seed[:, 0:ZN], 0.0).then_inc(S.s_msa, 1)
     g.wait_ge(S.s_msa, 1)
     g.remote_dma_fused(
-        [RemoteDMATransfer(dst_ids=_ids(topo, [nxt]), dma_engine_mask=mask, remote_sem=S.s_pad,
-                           srcs=[T.seed[:, 0:RUN - Q]], dsts=[T.ts[:, Q:RUN]], alu_op=0)],
+        [RemoteDMATransfer(dst_ids=_ids(topo, [nxt]), dma_engine_mask=_common_mask(topo, core, [nxt], NE_OFF),
+                           remote_sem=S.s_pad, srcs=[T.seed[:, 0:ZN]], dsts=[T.to[:, 0:ZN]], alu_op=0)],
         local_sem=S.s_sent)
 
-    ve.memset(T.wt[:, :], 0.0).then_inc(S.s_msw, 1)
-    sy.wait_ge(S.s_msw, 1)
-    sc.wait_ge(S.s_msw, 1)
     for a in range(NA):
-        for u in range(NU):
-            q = sc if u == 0 else sy
-            q.dma_start(T.wt[Q * a + PAD * R * u:Q * a + PAD * R * (u + 1):PAD, P * u:P * (u + 1)],
-                        T.vt[:, :]).then_inc(S.s_w, 16)
+        for q in range(NS):
+            dq = sc if q % 2 == 0 else sy
+            dq.dma_start(T.wt[Q * a + q:Q * (a + 1):NS, :], T.vt[:, :]).then_inc(S.s_w, 16)
 
     pe.wait_ge(S.s_v, 16)
     for u in range(NU):
         pe.wait_ge(S.s_x0 if u == 0 else S.s_x1, 16)
         for b in range(NBK):
-            o = UR * b + R * u
+            o = R * (NBK * u + b)
             pe.matmul(out=ps_t[:, o:o + R], lhsT=T.xs[:, HALF * u + b:HALF * (u + 1):NBK], rhs=T.vs[:, :],
                       start=True, stop=True).then_inc(S.s_pt, 1)
     ve.wait_ge(S.s_pt, NU * NBK)
@@ -167,26 +148,42 @@ def rank_program(g, core, T, topo):
 
     g.wait_ge(S.s_mine, 1)
     g.remote_dma_fused(
-        [RemoteDMATransfer(dst_ids=_ids(topo, hubs), dma_engine_mask=mask,
-                           remote_sem=S.s_arr, srcs=[T.mine[:, :]],
-                           dsts=[T.land[:, B * slot:B * (slot + 1)] for _h in hubs], alu_op=0)],
+        [RemoteDMATransfer(dst_ids=_ids(topo, fw), dma_engine_mask=_common_mask(topo, core, fw, NE_ON),
+                           remote_sem=S.s_arr, srcs=[T.mine[:, :]], dsts=[T.mine[:, :] for _h in fw], alu_op=0)],
         local_sem=S.s_sent)
-    g.wait_ge(S.s_sent, 2 * NE_RANK)
+    g.wait_ge(S.s_sent, NE_OFF + NE_ON)
 
-    ve.wait_ge(S.s_pad, NE_HUB * len(plan) + NE_RANK)
-    ve.wait_ge(S.s_got, NE_HUB * len(plan))
-    ve.tensor_tensor(out=T.ts[:, 0:RUN:PAD], in0=T.recv[:, 0:B], in1=T.recv[:, B:2 * B],
-                     op=AluOpType.add).then_inc(S.s_ts, 1)
-    ve.wait_ge(S.s_ts, 1)
-    ve.transpose(out=T.tt[:, :], in_=T.ts[:, :]).then_inc(S.s_tt, 1)
-
-    pe.wait_ge(S.s_w, 16 * NA * NU)
+    ve.wait_ge(S.s_pad, NE_OFF * (NS + 1))
+    ve.tensor_scalar(out=T.to[:, 0:W:NS], in0=ps_t[:, 0:B], scalar1=-2.0, scalar2=None,
+                     op0=AluOpType.mult).then_inc(S.s_to, 1)
+    ve.wait_ge(S.s_to, 1)
+    for u in range(NU):
+        ve.transpose(out=T.tto[:, RUN * u:RUN * (u + 1)], in_=T.to[:, RUN * u:RUN * (u + 1)]).then_inc(
+            S["s_tto%d" % u], 1)
+    pe.wait_ge(S.s_w, 16 * NA * NS)
     pe.wait_ge(S.s_mine, 1)
-    pe.wait_ge(S.s_tt, 1)
-    for z in range(NZ):
-        u, a = divmod(z, NA)
-        pe.matmul(out=T["ps%d" % z][:, 0:RUN], lhsT=T.wt[Q * a:Q * (a + 1), P * u:P * (u + 1)],
-                  rhs=T.tt[Q * a:Q * (a + 1), :], start=True, stop=True).then_inc(S["s_p%d" % z], 1)
+    for u in range(NU):
+        pe.wait_ge(S["s_tto%d" % u], 1)
+        for a in range(NA):
+            pe.matmul(out=T["ps%d" % (NA * u + a)][:, 0:RUN], lhsT=T.wt[Q * a:Q * (a + 1), :],
+                      rhs=T.tto[Q * a:Q * (a + 1), RUN * u:RUN * (u + 1)], start=True, stop=False)
+
+    for q in range(NS):
+        ve.wait_ge(S["s_g%d" % q], 2 * NE_OFF)
+        ve.tensor_tensor(out=T.ts[:, q:W:NS], in0=T.land[:, B * q:B * (q + 1)],
+                         in1=T.land[:, B * (q + NS):B * (q + NS + 1)], op=AluOpType.add).then_inc(S.s_ts, 1)
+    ve.wait_ge(S.s_ts, NS)
+    for u in range(NU):
+        ve.transpose(out=T.tt[:, RUN * u:RUN * (u + 1)], in_=T.ts[:, RUN * u:RUN * (u + 1)]).then_inc(
+            S["s_tt%d" % u], 1)
+
+    for u in range(NU):
+        pe.wait_ge(S["s_tt%d" % u], 1)
+        for a in range(NA):
+            z = NA * u + a
+            pe.matmul(out=T["ps%d" % z][:, 0:RUN], lhsT=T.wt[Q * a:Q * (a + 1), :],
+                      rhs=T.tt[Q * a:Q * (a + 1), RUN * u:RUN * (u + 1)], start=False, stop=True).then_inc(
+                S["s_p%d" % z], 1)
     ve.wait_ge(S.s_x0, 16)
     ve.wait_ge(S.s_x1, 16)
     per = NZ // PIECES

from concourse.bass import DstId, RemoteDMATransfer
from concourse.mybir import AluOpType

NS = 4
NE_ON = 16
NE_OFF = 8
R = 8
C = 512
P = 128
Q = 32
NA = P // Q
NU = 2
NBK = 2
B = NU * NBK * R
HALF = C // NU
W = NS * B
RUN = NBK * Q
NZ = C // RUN
PIECES = 4
ZN = Q
ZH = (W - ZN) // NS

SCRATCH = {
    "xs": ("sbuf", [P, C], "float32"),
    "vs": ("sbuf", [P, R], "float32"),
    "mine": ("sbuf", [P, B], "float32"),
    "land": ("sbuf", [P, 2 * NS * B], "float32"),
    "seed": ("sbuf", [P, Q], "float32"),
    "to": ("sbuf", [P, W], "float32"),
    "tto": ("sbuf", [P, W], "float32"),
    "ts": ("sbuf", [P, W], "float32"),
    "tt": ("sbuf", [P, W], "float32"),
    "wt": ("sbuf", [P, P], "float32"),
    "ys": ("sbuf", [P, C], "float32"),
}
for _z in range(NZ):
    SCRATCH["ps%d" % _z] = ("psum", [P, 512], "float32")
SEMAPHORES = (["s_v", "s_x0", "s_x1", "s_msa", "s_pad", "s_w", "s_pt", "s_mine", "s_sent", "s_arr", "s_to", "s_ts"]
              + ["s_tto%d" % u for u in range(NU)] + ["s_tt%d" % u for u in range(NU)]
              + ["s_g%d" % q for q in range(NS)] + ["s_p%d" % z for z in range(NZ)]
              + ["s_y%d" % k for k in range(PIECES)] + ["s_st%d" % k for k in range(PIECES)])


def _engines(mask, n):
    bits = [b for b in range(mask.bit_length()) if (mask >> b) & 1]
    step = len(bits) // n
    out = 0
    for b in bits[::step][:n]:
        out |= 1 << b
    return out


def _common_mask(topo, src, dsts, n):
    m = topo.mask(src, dsts[0])
    for d in dsts[1:]:
        m &= topo.mask(src, d)
    return _engines(m, n)


def _ids(topo, cores):
    out = []
    for c in cores:
        rid, pid, _se = topo.addr(c)
        out.append(DstId(rid=rid, pnc=pid))
    return out


def _forwarders(T, topo, c):
    ranks = list(T.cores)
    ok = [h for h in range(topo.CHIPS * topo.CORES_PER_CHIP)
          if topo.chip(h) == topo.chip(c) and h not in ranks and topo.may_write(c, h)
          and all(topo.may_write(h, d) for d in ranks)]
    near = [h for h in ok if topo.die(h) == topo.die(c)]
    far = [h for h in ok if topo.die(h) != topo.die(c)]
    half = NS // 2
    return near[:half] + far[:NS - half]


def _neighbour(T, topo, c):
    grp = [d for d in T.cores if d == c or (topo.may_write(c, d) and topo.may_write(d, c))]
    return grp[(grp.index(c) + 1) % len(grp)]


def _forwarder_program(g, core, T, topo, home, q):
    S = T.sem
    ranks = list(T.cores)
    n = len(ranks)
    i = ranks.index(home)
    offs = [o for o in range(1, n) if (o - 1) % NS == q]
    dests = [ranks[(i + o) % n] for o in offs]
    mask = _common_mask(topo, core, dests + [home], NE_OFF)
    lo = ZN + ZH * q
    g.vector.memset(T.seed[:, 0:ZH], 0.0).then_inc(S.s_msa, 1)
    g.wait_ge(S.s_msa, 1)
    g.remote_dma_fused(
        [RemoteDMATransfer(dst_ids=_ids(topo, [home]), dma_engine_mask=mask, remote_sem=S.s_pad,
                           srcs=[T.seed[:, 0:ZH]], dsts=[T.to[:, lo:lo + ZH]], alu_op=0)],
        local_sem=S.s_sent)
    g.wait_ge(S.s_arr, NE_ON)
    g.remote_dma_fused(
        [RemoteDMATransfer(dst_ids=_ids(topo, dests), dma_engine_mask=mask, remote_sem=S["s_g%d" % q],
                           srcs=[T.mine[:, :]], dsts=[T.land[:, B * (o - 1):B * o] for o in offs], alu_op=0)],
        local_sem=S.s_sent)
    g.wait_ge(S.s_sent, 2 * NE_OFF)


def rank_program(g, core, T, topo):
    for c in T.cores:
        if topo.chip(c) == topo.chip(core) and c != core:
            fw = _forwarders(T, topo, c)
            if core in fw:
                _forwarder_program(g, core, T, topo, c, fw.index(core))
            return
    if T.rank_of(core) is None:
        return
    S = T.sem
    fw = _forwarders(T, topo, core)
    nxt = _neighbour(T, topo, core)
    sy, sc, ve, pe = g.sync, g.scalar, g.vector, g.tensor
    ps_t = T["ps%d" % (NZ - 1)]

    sc.dma_start(T.xs[:, 0:HALF], T.x[:, 0:HALF]).then_inc(S.s_x0, 16)
    sy.dma_start(T.vs[:, :], T.v[:, :]).then_inc(S.s_v, 16)
    sy.dma_start(T.xs[:, HALF:C], T.x[:, HALF:C]).then_inc(S.s_x1, 16)

    ve.memset(T.seed[:, 0:ZN], 0.0).then_inc(S.s_msa, 1)
    g.wait_ge(S.s_msa, 1)
    g.remote_dma_fused(
        [RemoteDMATransfer(dst_ids=_ids(topo, [nxt]), dma_engine_mask=_common_mask(topo, core, [nxt], NE_OFF),
                           remote_sem=S.s_pad, srcs=[T.seed[:, 0:ZN]], dsts=[T.to[:, 0:ZN]], alu_op=0)],
        local_sem=S.s_sent)

    for a in range(NA):
        for q in range(NS):
            dq = sc if q % 2 == 0 else sy
            dq.dma_start(T.wt[Q * a + q:Q * (a + 1):NS, :], T.vt[:, :]).then_inc(S.s_w, 16)

    pe.wait_ge(S.s_v, 16)
    for u in range(NU):
        pe.wait_ge(S.s_x0 if u == 0 else S.s_x1, 16)
        for b in range(NBK):
            o = R * (NBK * u + b)
            pe.matmul(out=ps_t[:, o:o + R], lhsT=T.xs[:, HALF * u + b:HALF * (u + 1):NBK], rhs=T.vs[:, :],
                      start=True, stop=True).then_inc(S.s_pt, 1)
    ve.wait_ge(S.s_pt, NU * NBK)
    ve.tensor_scalar(out=T.mine[:, :], in0=ps_t[:, 0:B], scalar1=-2.0, scalar2=None,
                     op0=AluOpType.mult).then_inc(S.s_mine, 1)

    g.wait_ge(S.s_mine, 1)
    g.remote_dma_fused(
        [RemoteDMATransfer(dst_ids=_ids(topo, fw), dma_engine_mask=_common_mask(topo, core, fw, NE_ON),
                           remote_sem=S.s_arr, srcs=[T.mine[:, :]], dsts=[T.mine[:, :] for _h in fw], alu_op=0)],
        local_sem=S.s_sent)
    g.wait_ge(S.s_sent, NE_OFF + NE_ON)

    ve.wait_ge(S.s_pad, NE_OFF * (NS + 1))
    ve.tensor_scalar(out=T.to[:, 0:W:NS], in0=ps_t[:, 0:B], scalar1=-2.0, scalar2=None,
                     op0=AluOpType.mult).then_inc(S.s_to, 1)
    ve.wait_ge(S.s_to, 1)
    for u in range(NU):
        ve.transpose(out=T.tto[:, RUN * u:RUN * (u + 1)], in_=T.to[:, RUN * u:RUN * (u + 1)]).then_inc(
            S["s_tto%d" % u], 1)
    pe.wait_ge(S.s_w, 16 * NA * NS)
    pe.wait_ge(S.s_mine, 1)
    for u in range(NU):
        pe.wait_ge(S["s_tto%d" % u], 1)
        for a in range(NA):
            pe.matmul(out=T["ps%d" % (NA * u + a)][:, 0:RUN], lhsT=T.wt[Q * a:Q * (a + 1), :],
                      rhs=T.tto[Q * a:Q * (a + 1), RUN * u:RUN * (u + 1)], start=True, stop=False)

    for q in range(NS):
        ve.wait_ge(S["s_g%d" % q], 2 * NE_OFF)
        ve.tensor_tensor(out=T.ts[:, q:W:NS], in0=T.land[:, B * q:B * (q + 1)],
                         in1=T.land[:, B * (q + NS):B * (q + NS + 1)], op=AluOpType.add).then_inc(S.s_ts, 1)
    ve.wait_ge(S.s_ts, NS)
    for u in range(NU):
        ve.transpose(out=T.tt[:, RUN * u:RUN * (u + 1)], in_=T.ts[:, RUN * u:RUN * (u + 1)]).then_inc(
            S["s_tt%d" % u], 1)

    for u in range(NU):
        pe.wait_ge(S["s_tt%d" % u], 1)
        for a in range(NA):
            z = NA * u + a
            pe.matmul(out=T["ps%d" % z][:, 0:RUN], lhsT=T.wt[Q * a:Q * (a + 1), :],
                      rhs=T.tt[Q * a:Q * (a + 1), RUN * u:RUN * (u + 1)], start=False, stop=True).then_inc(
                S["s_p%d" % z], 1)
    ve.wait_ge(S.s_x0, 16)
    ve.wait_ge(S.s_x1, 16)
    per = NZ // PIECES
    w = C // PIECES
    for z in range(NZ):
        k = z // per
        ve.wait_ge(S["s_p%d" % z], 1)
        for b in range(NBK):
            ve.tensor_tensor(out=T.ys[:, RUN * z + b:RUN * (z + 1):NBK], in0=T.xs[:, RUN * z + b:RUN * (z + 1):NBK],
                             in1=T["ps%d" % z][:, Q * b:Q * (b + 1)], op=AluOpType.add).then_inc(S["s_y%d" % k], 1)
    for k in range(PIECES):
        q = sy if k % 2 == 0 else sc
        q.wait_ge(S["s_y%d" % k], per * NBK)
        q.dma_start(T.y[:, w * k:w * (k + 1)], T.ys[:, w * k:w * (k + 1)]).then_inc(S["s_st%d" % k], 16)
    for k in range(PIECES):
        q = sy if k % 2 == 0 else sc
        q.wait_ge(S["s_st%d" % k], 16)
